import numpy as np
import ml_dtypes


def mxq(x, axis, fmt="e4m3"):
    dtype, down = {"e4m3": (ml_dtypes.float8_e4m3fn, 7), "e5m2": (ml_dtypes.float8_e5m2, 14)}[fmt]
    v = np.moveaxis(np.asarray(x, np.float32).astype(ml_dtypes.bfloat16).astype(np.float64), axis, -1)
    blocks = v.reshape(v.shape[:-1] + (-1, 32))
    amax = np.abs(blocks).max(-1, keepdims=True)
    byte = np.maximum(np.where(amax > 0, np.frexp(amax)[1] - 1 + 127, 0) - down, 1)
    scale = np.exp2(byte - 127.0)
    codes = (blocks / scale).astype(np.float32).astype(dtype).astype(np.float64)
    return np.moveaxis((codes * scale).reshape(v.shape), -1, axis)


WIDE = False


def mx_kscale(k):
    if not WIDE:
        return np.ones(k)
    levels = np.array([10, -10, 5, -5, 0])
    if k % 512:
        return np.exp2(np.random.permutation(np.resize(levels, k // 32))).repeat(32)
    a = np.empty((k // 512, 16))
    for p in range(k // 512):
        a[p, :8] = np.random.permutation(np.resize(levels, 8))
        for g in range(8):
            far = levels[np.abs(levels - a[p, g]) >= 10]
            a[p, g + 8] = far[np.random.randint(len(far))]
    return np.exp2(a.ravel()).repeat(32)


def f64(x):
    return np.asarray(x).astype(np.float64)


def striped8(idx):
    return np.asarray(idx).reshape(8, -1, 16).transpose(0, 2, 1).reshape(128, -1).astype(np.uint16)


def unstriped8(offs):
    return offs.reshape(8, 16, -1).transpose(0, 2, 1).reshape(8, -1).astype(np.int64)


def pick8(x, idx, run):
    r = np.arange(len(x))
    return x[r[:, None], idx[r % (8 * run) // run]]


E2M1 = np.array([0.0, 0.5, 1.0, 1.5, 2.0, 3.0, 4.0, 6.0, -0.0, -0.5, -1.0, -1.5, -2.0, -3.0, -4.0, -6.0])


def pack_weight(w, fmt):
    k, n = w.shape
    w = f64(np.asarray(w, np.float32).astype(ml_dtypes.bfloat16)).reshape(k // 32, 32, n)
    amax = np.abs(w).max(1)
    if fmt == "e4m3":
        byte = np.frexp(amax)[1] - 1 + 127 - 7
    else:
        mant, ex = np.frexp(amax / 6.0)
        byte = np.where(mant > 0.5, ex, ex - 1) + 127
    byte = np.clip(np.where(amax > 0, byte, 1), 1, 254)
    scaled = (w * np.exp2(127.0 - byte)[:, None, :]).reshape(k, n).astype(np.float32)
    by_word = np.ascontiguousarray(scaled.reshape(k // 512, 128, 4, n).transpose(0, 1, 3, 2))
    if fmt == "e4m3":
        words = by_word.astype(ml_dtypes.float8_e4m3fn).view(np.uint8)
    else:
        c = by_word.astype(ml_dtypes.float4_e2m1fn).view(np.uint8) & 0xF
        words = (c[..., 0::2] | (c[..., 1::2] << 4)).reshape(k // 512, 128, 2 * n)
    return np.ascontiguousarray(words), np.ascontiguousarray(byte.astype(np.uint8).reshape(k // 512, 16, n))


def unpack_weight(words, scales, fmt):
    g, _, n = scales.shape
    words = np.ascontiguousarray(words).reshape(g, 128, n, -1)
    if fmt == "e4m3":
        vals = words.view(ml_dtypes.float8_e4m3fn).astype(np.float64)
    else:
        nib = np.empty((g, 128, n, 4), np.uint8)
        nib[..., 0::2] = words & 0xF
        nib[..., 1::2] = words >> 4
        vals = E2M1[nib]
    vals = vals * np.repeat(np.exp2(scales.astype(np.float64) - 127.0), 8, axis=1)[..., None]
    return vals.transpose(0, 1, 3, 2).reshape(g * 512, n)


D, K, T, U, X, I, Q = 512, 512, 1024, 1024, 1024, 512, 128


def setup_inputs():
    n = np.random.standard_normal
    idx = np.stack([np.random.permutation(T)[:I] for _ in range(8)])
    idx2 = np.stack([np.random.permutation(U)[:I] for _ in range(8)])
    idx3 = np.stack([np.random.permutation(U)[:I] for _ in range(8)])
    idx4 = np.stack([np.random.permutation(X)[:I] for _ in range(8)])
    idx5 = np.stack([np.random.permutation(X)[:I] for _ in range(8)])
    idx6 = np.stack([np.random.permutation(T)[:I] for _ in range(8)])
    fd = mx_kscale(D)
    fk = mx_kscale(K)
    wqp = pack_weight(n((D, K)) * 1.0 / np.sqrt(D) * fd[:, None] * fk, "e4m3")
    keysp = pack_weight(n((K, T)) * 1.0 / np.sqrt(K) / fk[:, None], "e2m1")
    notesp = pack_weight(n((K, U)) * 1.0 / np.sqrt(K) / fk[:, None], "e4m3")
    usersp = pack_weight(n((D, X)) * 1.0 / np.sqrt(D) * fd[:, None], "e2m1")
    return {
        "states": (n((D, Q)) * 0.95 / fd[:, None]).astype(np.float32),
        "wq_words": wqp[0],
        "wq_scales": wqp[1],
        "keys_words": keysp[0],
        "keys_scales": keysp[1],
        "notes_words": notesp[0],
        "notes_scales": notesp[1],
        "users_words": usersp[0],
        "users_scales": usersp[1],
        "offs": striped8(idx),
        "offs2": striped8(idx2),
        "offs3": striped8(idx3),
        "offs4": striped8(idx4),
        "offs5": striped8(idx5),
        "offs6": striped8(idx6),
    }


def reference(states, wq_words, wq_scales, keys_words, keys_scales, notes_words, notes_scales, users_words, users_scales, offs, offs2, offs3, offs4, offs5, offs6):
    idx = unstriped8(offs)
    idx2 = unstriped8(offs2)
    idx3 = unstriped8(offs3)
    idx4 = unstriped8(offs4)
    idx5 = unstriped8(offs5)
    idx6 = unstriped8(offs6)
    wqu = unpack_weight(wq_words, wq_scales, "e4m3")
    keysu = unpack_weight(keys_words, keys_scales, "e2m1")
    notesu = unpack_weight(notes_words, notes_scales, "e4m3")
    usersu = unpack_weight(users_words, users_scales, "e2m1")
    statesq = mxq(f64(states), 0, "e4m3")
    qv = wqu.T @ statesq
    qvq = mxq(qv, 0, "e4m3")
    a = qvq.T @ keysu
    b = qvq.T @ notesu
    c0 = statesq.T @ usersu
    f1 = np.zeros((Q, U))
    f1[np.arange(Q)[:, None], idx2[np.arange(Q) % 128 // 16]] = pick8(a, idx, 16)
    bb = b + f1
    f2 = np.zeros((Q, X))
    f2[np.arange(Q)[:, None], idx4[np.arange(Q) % 128 // 16]] = pick8(bb, idx3, 16)
    cc = c0 + f2
    f3 = np.zeros((Q, T))
    f3[np.arange(Q)[:, None], idx6[np.arange(Q) % 128 // 16]] = pick8(cc, idx5, 16)
    aa = a - f3
    y = pick8(aa, idx, 16)
    return y

@@ -1,0 +1,147 @@
+from contextlib import ExitStack
+
+import concourse.mybir as mybir
+
+D, K, T, I, Q = 512, 512, 1024, 512, 128
+FLOPS = 2 * D * K * Q + 3 * 2 * K * Q * T
+
+F32 = mybir.dt.float32
+BF16 = mybir.dt.bfloat16
+I32 = mybir.dt.int32
+U32 = mybir.dt.uint32
+U16 = mybir.dt.uint16
+U8 = mybir.dt.uint8
+FP8X4 = mybir.dt.float8_e4m3fn_x4
+FP4X4 = mybir.dt.float4_e2m1fn_x4
+COPY = mybir.ActivationFunctionType.Copy
+ADD = mybir.AluOpType.add
+SUB = mybir.AluOpType.subtract
+
+P = 128
+PACK = 4
+BANK = 512
+HALF = I // 2
+LIST_COLS = I // 16
+HALF_COLS = HALF // 16
+
+
+def tile_attend_triangle_madethree_kernel(tc, states, wq_words, wq_scales, keys_words, keys_scales, notes_words,
+                                           notes_scales, users_words, users_scales, offs, offs2, offs3, offs4,
+                                           offs5, offs6, out):
+    nc = tc.nc
+    with ExitStack() as ctx:
+        sb = ctx.enter_context(tc.tile_pool(name="sb", bufs=1))
+        ps = ctx.enter_context(tc.psum_pool(name="ps", bufs=1))
+
+        def plane(name, width, eng):
+            t = sb.tile([P, width], U8, name=name, align_bytes=64)
+            eng.memset(t[:].bitcast(I32), 0)
+            return t
+
+        def load_plane(t, scales):
+            for g in range(4):
+                nc.sync.dma_start(out=t[32 * g:32 * g + 4, :].bitcast(I32),
+                                  in_=scales[0, 4 * g:4 * g + 4, :].bitcast(I32))
+
+        def load_list(name, src):
+            t = sb.tile([P, LIST_COLS], U16, name=name)
+            nc.sync.dma_start(t[:], src)
+            return t
+
+        wq_raw_plane = plane("wq_raw_plane", K, nc.vector)
+        keys_plane = plane("keys_plane", T, nc.vector)
+        notes_plane = plane("notes_plane", T, nc.gpsimd)
+        users_plane = plane("users_plane", T, nc.gpsimd)
+        fills = []
+        for h in range(3):
+            f = sb.tile([P, T], F32, name="fill%d" % h)
+            (nc.vector if h == 0 else nc.gpsimd).memset(f[:], 0.0)
+            fills.append(f)
+
+        st_raw = sb.tile([P, PACK, Q], F32, name="st_raw")
+        nc.scalar.dma_start(out=st_raw[:], in_=states.rearrange("(p j) q -> p j q", j=PACK))
+        wq_raw = sb.tile([P, K], U32, name="wq_raw")
+        nc.sync.dma_start(out=wq_raw[:].bitcast(I32), in_=wq_words[0].rearrange("p n t -> p (n t)").bitcast(I32))
+        load_plane(wq_raw_plane, wq_scales)
+        keys = sb.tile([P, 2 * T], U8, name="keys", align_bytes=64)
+        nc.sync.dma_start(out=keys[:].bitcast(I32), in_=keys_words[0].bitcast(I32))
+        load_plane(keys_plane, keys_scales)
+        l1 = load_list("l1", offs)
+        l2 = load_list("l2", offs2)
+        notes = sb.tile([P, T], U32, name="notes", align_bytes=64)
+        nc.sync.dma_start(out=notes[:].bitcast(I32), in_=notes_words[0].rearrange("p n t -> p (n t)").bitcast(I32))
+        load_plane(notes_plane, notes_scales)
+        l3 = load_list("l3", offs3)
+        l4 = load_list("l4", offs4)
+        users = sb.tile([P, 2 * T], U8, name="users", align_bytes=64)
+        nc.sync.dma_start(out=users[:].bitcast(I32), in_=users_words[0].bitcast(I32))
+        load_plane(users_plane, users_scales)
+        l5 = load_list("l5", offs5)
+        l6 = load_list("l6", offs6)
+
+        wq_plane = sb.tile([P, K], U8, name="wq_plane", align_bytes=64)
+        nc.vector.tensor_copy(out=wq_plane[:].rearrange("p (t m) -> p t m", t=PACK),
+                              in_=wq_raw_plane[:].rearrange("p (m t) -> p t m", t=PACK))
+        wq = sb.tile([P, K], U32, name="wq", align_bytes=64)
+        nc.scalar.copy(out=wq[:].rearrange("p (t m) -> p t m", t=PACK),
+                       in_=wq_raw[:].rearrange("p (m t) -> p t m", t=PACK))
+
+        st_bf = sb.tile([P, Q, PACK], BF16, name="st_bf", align_bytes=64)
+        nc.vector.tensor_copy(out=st_bf[:], in_=st_raw[:].rearrange("p j q -> p q j"))
+        st_q = sb.tile([P, Q], U32, name="st_q", align_bytes=64)
+        st_s = sb.tile([P, Q], U8, name="st_s", align_bytes=64)
+        nc.vector.quantize_mx(out=st_q[:].bitcast(FP8X4), scales=st_s[:], in_=st_bf[:].rearrange("p q j -> p (q j)"))
+
+        qv_ps = ps.tile([P, PACK, Q], F32, name="qv_ps", tag="qv_ps")
+        for t in range(PACK):
+            cols = slice(t * P, (t + 1) * P)
+            nc.tensor.matmul_mx(out=qv_ps[:, t, :], lhsT=wq[:, cols].bitcast(FP8X4), lhsT_scale=wq_plane[:, cols],
+                                rhs=st_q[:].bitcast(FP8X4), rhs_scale=st_s[:], start=True, stop=True)
+        qv_bf = sb.tile([P, Q, PACK], BF16, name="qv_bf", align_bytes=64)
+        nc.vector.tensor_copy(out=qv_bf[:], in_=qv_ps[:].rearrange("p t q -> p q t"))
+        qv_q = sb.tile([P, Q], U32, name="qv_q", align_bytes=64)
+        qv_s = sb.tile([P, Q], U8, name="qv_s", align_bytes=64)
+        nc.vector.quantize_mx(out=qv_q[:].bitcast(FP8X4), scales=qv_s[:], in_=qv_bf[:].rearrange("p q j -> p (q j)"))
+
+        def scores(tags, n, lq, ls, words, bytes_a_col, dt, pl):
+            banks = []
+            for h in range(T // n):
+                bank = ps.tile([P, n], F32, name=tags[h], tag=tags[h])
+                nc.tensor.matmul_mx(out=bank[:], lhsT=lq[:].bitcast(FP8X4), lhsT_scale=ls[:],
+                                    rhs=words[:, h * n * bytes_a_col:(h + 1) * n * bytes_a_col].bitcast(dt),
+                                    rhs_scale=pl[:, h * n:(h + 1) * n], start=True, stop=True)
+                banks.append(bank)
+            return banks
+
+        a_ps = scores(["a0", "a1", "a2", "a3"], 256, qv_q, qv_s, keys, 2, FP4X4, keys_plane)
+        a_sb = sb.tile([P, T], F32, name="a_sb")
+        for j in range(4):
+            cols = slice(j * 256, (j + 1) * 256)
+            if j % 2 == 0:
+                nc.scalar.activation(a_sb[:, cols], a_ps[j][:], COPY)
+            else:
+                nc.vector.tensor_copy(out=a_sb[:, cols], in_=a_ps[j][:])
+        b_ps = scores(["b0", "b1"], BANK, qv_q, qv_s, notes, 1, FP8X4, notes_plane)
+        c_ps = scores(["c0", "qv_ps"], BANK, st_q, st_s, users, 2, FP4X4, users_plane)
+
+        def pick(name, window, lst):
+            picked = sb.tile([P, I], F32, name=name)
+            nc.vector.tensor_copy(picked[:, 0:HALF], window[:].indirect(lst[:, 0:HALF_COLS]))
+            nc.scalar.activation(picked[:, HALF:I], window[:].indirect(lst[:, HALF_COLS:LIST_COLS]), COPY)
+            return picked
+
+        window = a_sb
+        hops = ((l1, l2, b_ps), (l3, l4, c_ps), (l5, l6, None))
+        for h, (src_list, dst_list, base) in enumerate(hops):
+            picked = pick("pick%d" % h, window, src_list)
+            nc.vector.tensor_copy(fills[h][:].indirect(dst_list[:]), picked[:])
+            window = sb.tile([P, T], F32, name="sum%d" % h)
+            if base is None:
+                nc.vector.tensor_tensor(window[:], a_sb[:], fills[h][:], SUB)
+            else:
+                for j in range(T // BANK):
+                    cols = slice(j * BANK, (j + 1) * BANK)
+                    nc.vector.tensor_tensor(window[:, cols], base[j][:], fills[h][:, cols], ADD)
+        res = pick("res", window, l1)
+        nc.sync.dma_start(out=out[:, 0:HALF], in_=res[:, 0:HALF])
+        nc.scalar.dma_start(out=out[:, HALF:I], in_=res[:, HALF:I])

@@ -20,6 +20,7 @@ SUB = mybir.AluOpType.subtract
 P = 128
 PACK = 4
 BANK = 512
+SPLIT = 704
 HALF = I // 2
 LIST_COLS = I // 16
 HALF_COLS = HALF // 16
@@ -38,9 +39,9 @@ def tile_attend_triangle_madethree_kernel(tc, states, wq_words, wq_scales, keys_
             eng.memset(t[:].bitcast(I32), 0)
             return t
 
-        def load_plane(t, scales):
+        def load_plane(t, scales, queue=nc.sync):
             for g in range(4):
-                nc.sync.dma_start(out=t[32 * g:32 * g + 4, :].bitcast(I32),
+                queue.dma_start(out=t[32 * g:32 * g + 4, :].bitcast(I32),
                                   in_=scales[0, 4 * g:4 * g + 4, :].bitcast(I32))
 
         def load_list(name, src):
@@ -48,10 +49,10 @@ def tile_attend_triangle_madethree_kernel(tc, states, wq_words, wq_scales, keys_
             nc.sync.dma_start(t[:], src)
             return t
 
-        wq_raw_plane = plane("wq_raw_plane", K, nc.vector)
-        keys_plane = plane("keys_plane", T, nc.vector)
-        notes_plane = plane("notes_plane", T, nc.gpsimd)
-        users_plane = plane("users_plane", T, nc.gpsimd)
+        wq_raw_plane = plane("wq_raw_plane", K, nc.gpsimd)
+        keys_plane = plane("keys_plane", T, nc.gpsimd)
+        notes_plane = plane("notes_plane", T, nc.vector)
+        users_plane = plane("users_plane", T, nc.vector)
         fills = []
         for h in range(3):
             f = sb.tile([P, T], F32, name="fill%d" % h)
@@ -59,10 +60,10 @@ def tile_attend_triangle_madethree_kernel(tc, states, wq_words, wq_scales, keys_
             fills.append(f)
 
         st_raw = sb.tile([P, PACK, Q], F32, name="st_raw")
-        nc.scalar.dma_start(out=st_raw[:], in_=states.rearrange("(p j) q -> p j q", j=PACK))
+        nc.sync.dma_start(out=st_raw[:], in_=states.rearrange("(p j) q -> p j q", j=PACK))
         wq_raw = sb.tile([P, K], U32, name="wq_raw")
         nc.sync.dma_start(out=wq_raw[:].bitcast(I32), in_=wq_words[0].rearrange("p n t -> p (n t)").bitcast(I32))
-        load_plane(wq_raw_plane, wq_scales)
+        load_plane(wq_raw_plane, wq_scales, nc.scalar)
         keys = sb.tile([P, 2 * T], U8, name="keys", align_bytes=64)
         nc.sync.dma_start(out=keys[:].bitcast(I32), in_=keys_words[0].bitcast(I32))
         load_plane(keys_plane, keys_scales)
@@ -79,23 +80,21 @@ def tile_attend_triangle_madethree_kernel(tc, states, wq_words, wq_scales, keys_
         l5 = load_list("l5", offs5)
         l6 = load_list("l6", offs6)
 
-        wq_plane = sb.tile([P, K], U8, name="wq_plane", align_bytes=64)
-        nc.vector.tensor_copy(out=wq_plane[:].rearrange("p (t m) -> p t m", t=PACK),
-                              in_=wq_raw_plane[:].rearrange("p (m t) -> p t m", t=PACK))
-        wq = sb.tile([P, K], U32, name="wq", align_bytes=64)
-        nc.scalar.copy(out=wq[:].rearrange("p (t m) -> p t m", t=PACK),
-                       in_=wq_raw[:].rearrange("p (m t) -> p t m", t=PACK))
-
         st_bf = sb.tile([P, Q, PACK], BF16, name="st_bf", align_bytes=64)
-        nc.vector.tensor_copy(out=st_bf[:], in_=st_raw[:].rearrange("p j q -> p q j"))
+        nc.vector.tensor_copy(out=st_bf[:].rearrange("p (c i) j -> p c j i", i=4),
+                              in_=st_raw[:].rearrange("p j (c i) -> p c j i", i=4))
+        wq_plane = sb.tile([P, PACK, P], U8, name="wq_plane", align_bytes=64)
+        wq = sb.tile([P, PACK, P], U32, name="wq", align_bytes=64)
+        for t in range(PACK):
+            nc.vector.tensor_copy(out=wq_plane[:, t, :], in_=wq_raw_plane[:, t::PACK])
+            nc.scalar.copy(out=wq[:, t, :], in_=wq_raw[:, t::PACK])
         st_q = sb.tile([P, Q], U32, name="st_q", align_bytes=64)
         st_s = sb.tile([P, Q], U8, name="st_s", align_bytes=64)
         nc.vector.quantize_mx(out=st_q[:].bitcast(FP8X4), scales=st_s[:], in_=st_bf[:].rearrange("p q j -> p (q j)"))
 
         qv_ps = ps.tile([P, PACK, Q], F32, name="qv_ps", tag="qv_ps")
         for t in range(PACK):
-            cols = slice(t * P, (t + 1) * P)
-            nc.tensor.matmul_mx(out=qv_ps[:, t, :], lhsT=wq[:, cols].bitcast(FP8X4), lhsT_scale=wq_plane[:, cols],
+            nc.tensor.matmul_mx(out=qv_ps[:, t, :], lhsT=wq[:, t, :].bitcast(FP8X4), lhsT_scale=wq_plane[:, t, :],
                                 rhs=st_q[:].bitcast(FP8X4), rhs_scale=st_s[:], start=True, stop=True)
         qv_bf = sb.tile([P, Q, PACK], BF16, name="qv_bf", align_bytes=64)
         nc.vector.tensor_copy(out=qv_bf[:], in_=qv_ps[:].rearrange("p t q -> p q t"))
@@ -130,18 +129,23 @@ def tile_attend_triangle_madethree_kernel(tc, states, wq_words, wq_scales, keys_
             nc.scalar.activation(picked[:, HALF:I], window[:].indirect(lst[:, HALF_COLS:LIST_COLS]), COPY)
             return picked
 
+        def tail_in_sbuf(name, banks):
+            t = sb.tile([P, T - SPLIT], F32, name=name)
+            nc.scalar.activation(t[:], banks[1][:, SPLIT - BANK:BANK], COPY)
+            return t[:]
+
         window = a_sb
-        hops = ((l1, l2, b_ps), (l3, l4, c_ps), (l5, l6, None))
-        for h, (src_list, dst_list, base) in enumerate(hops):
+        for h, (src_list, dst_list) in enumerate(((l1, l2), (l3, l4), (l5, l6))):
             picked = pick("pick%d" % h, window, src_list)
+            banks, op = ((b_ps, ADD), (c_ps, ADD), (a_ps, SUB))[h]
+            tail = a_sb[:, SPLIT:T] if banks is a_ps else tail_in_sbuf("tail%d" % h, banks)
             nc.vector.tensor_copy(fills[h][:].indirect(dst_list[:]), picked[:])
             window = sb.tile([P, T], F32, name="sum%d" % h)
-            if base is None:
-                nc.vector.tensor_tensor(window[:], a_sb[:], fills[h][:], SUB)
-            else:
-                for j in range(T // BANK):
-                    cols = slice(j * BANK, (j + 1) * BANK)
-                    nc.vector.tensor_tensor(window[:, cols], base[j][:], fills[h][:, cols], ADD)
+            nc.gpsimd.tensor_tensor(window[:, SPLIT:T], tail, fills[h][:, SPLIT:T], op)
+            width = T // len(banks)
+            for c0 in range(0, SPLIT, width):
+                c1 = min(c0 + width, SPLIT)
+                nc.vector.tensor_tensor(window[:, c0:c1], banks[c0 // width][:, 0:c1 - c0], fills[h][:, c0:c1], op)
         res = pick("res", window, l1)
         nc.sync.dma_start(out=out[:, 0:HALF], in_=res[:, 0:HALF])
         nc.scalar.dma_start(out=out[:, HALF:I], in_=res[:, HALF:I])

@@ -56,7 +56,7 @@ def tile_attend_triangle_madethree_kernel(tc, states, wq_words, wq_scales, keys_
         fills = []
         for h in range(3):
             f = sb.tile([P, T], F32, name="fill%d" % h)
-            (nc.vector if h == 0 else nc.gpsimd).memset(f[:], 0.0)
+            nc.vector.memset(f[:], 0.0)
             fills.append(f)
 
         st_raw = sb.tile([P, PACK, Q], F32, name="st_raw")

from contextlib import ExitStack

import concourse.mybir as mybir

D, K, T, I, Q = 512, 512, 1024, 512, 128
FLOPS = 2 * D * K * Q + 3 * 2 * K * Q * T

F32 = mybir.dt.float32
BF16 = mybir.dt.bfloat16
I32 = mybir.dt.int32
U32 = mybir.dt.uint32
U16 = mybir.dt.uint16
U8 = mybir.dt.uint8
FP8X4 = mybir.dt.float8_e4m3fn_x4
FP4X4 = mybir.dt.float4_e2m1fn_x4
COPY = mybir.ActivationFunctionType.Copy
ADD = mybir.AluOpType.add
SUB = mybir.AluOpType.subtract

P = 128
PACK = 4
BANK = 512
SPLIT = 704
HALF = I // 2
LIST_COLS = I // 16
HALF_COLS = HALF // 16


def tile_attend_triangle_madethree_kernel(tc, states, wq_words, wq_scales, keys_words, keys_scales, notes_words,
                                           notes_scales, users_words, users_scales, offs, offs2, offs3, offs4,
                                           offs5, offs6, out):
    nc = tc.nc
    with ExitStack() as ctx:
        sb = ctx.enter_context(tc.tile_pool(name="sb", bufs=1))
        ps = ctx.enter_context(tc.psum_pool(name="ps", bufs=1))

        def plane(name, width, eng):
            t = sb.tile([P, width], U8, name=name, align_bytes=64)
            eng.memset(t[:].bitcast(I32), 0)
            return t

        def load_plane(t, scales, queue=nc.sync):
            for g in range(4):
                queue.dma_start(out=t[32 * g:32 * g + 4, :].bitcast(I32),
                                  in_=scales[0, 4 * g:4 * g + 4, :].bitcast(I32))

        def load_list(name, src):
            t = sb.tile([P, LIST_COLS], U16, name=name)
            nc.sync.dma_start(t[:], src)
            return t

        wq_raw_plane = plane("wq_raw_plane", K, nc.gpsimd)
        keys_plane = plane("keys_plane", T, nc.gpsimd)
        notes_plane = plane("notes_plane", T, nc.vector)
        users_plane = plane("users_plane", T, nc.vector)
        fills = []
        for h in range(3):
            f = sb.tile([P, T], F32, name="fill%d" % h)
            nc.vector.memset(f[:], 0.0)
            fills.append(f)

        st_raw = sb.tile([P, PACK, Q], F32, name="st_raw")
        nc.sync.dma_start(out=st_raw[:], in_=states.rearrange("(p j) q -> p j q", j=PACK))
        wq_raw = sb.tile([P, K], U32, name="wq_raw")
        nc.sync.dma_start(out=wq_raw[:].bitcast(I32), in_=wq_words[0].rearrange("p n t -> p (n t)").bitcast(I32))
        load_plane(wq_raw_plane, wq_scales, nc.scalar)
        keys = sb.tile([P, 2 * T], U8, name="keys", align_bytes=64)
        nc.sync.dma_start(out=keys[:].bitcast(I32), in_=keys_words[0].bitcast(I32))
        load_plane(keys_plane, keys_scales)
        l1 = load_list("l1", offs)
        l2 = load_list("l2", offs2)
        notes = sb.tile([P, T], U32, name="notes", align_bytes=64)
        nc.sync.dma_start(out=notes[:].bitcast(I32), in_=notes_words[0].rearrange("p n t -> p (n t)").bitcast(I32))
        load_plane(notes_plane, notes_scales)
        l3 = load_list("l3", offs3)
        l4 = load_list("l4", offs4)
        users = sb.tile([P, 2 * T], U8, name="users", align_bytes=64)
        nc.sync.dma_start(out=users[:].bitcast(I32), in_=users_words[0].bitcast(I32))
        load_plane(users_plane, users_scales)
        l5 = load_list("l5", offs5)
        l6 = load_list("l6", offs6)

        st_bf = sb.tile([P, Q, PACK], BF16, name="st_bf", align_bytes=64)
        nc.vector.tensor_copy(out=st_bf[:].rearrange("p (c i) j -> p c j i", i=4),
                              in_=st_raw[:].rearrange("p j (c i) -> p c j i", i=4))
        wq_plane = sb.tile([P, PACK, P], U8, name="wq_plane", align_bytes=64)
        wq = sb.tile([P, PACK, P], U32, name="wq", align_bytes=64)
        for t in range(PACK):
            nc.vector.tensor_copy(out=wq_plane[:, t, :], in_=wq_raw_plane[:, t::PACK])
            nc.scalar.copy(out=wq[:, t, :], in_=wq_raw[:, t::PACK])
        st_q = sb.tile([P, Q], U32, name="st_q", align_bytes=64)
        st_s = sb.tile([P, Q], U8, name="st_s", align_bytes=64)
        nc.vector.quantize_mx(out=st_q[:].bitcast(FP8X4), scales=st_s[:], in_=st_bf[:].rearrange("p q j -> p (q j)"))

        qv_ps = ps.tile([P, PACK, Q], F32, name="qv_ps", tag="qv_ps")
        for t in range(PACK):
            nc.tensor.matmul_mx(out=qv_ps[:, t, :], lhsT=wq[:, t, :].bitcast(FP8X4), lhsT_scale=wq_plane[:, t, :],
                                rhs=st_q[:].bitcast(FP8X4), rhs_scale=st_s[:], start=True, stop=True)
        qv_bf = sb.tile([P, Q, PACK], BF16, name="qv_bf", align_bytes=64)
        nc.vector.tensor_copy(out=qv_bf[:], in_=qv_ps[:].rearrange("p t q -> p q t"))
        qv_q = sb.tile([P, Q], U32, name="qv_q", align_bytes=64)
        qv_s = sb.tile([P, Q], U8, name="qv_s", align_bytes=64)
        nc.vector.quantize_mx(out=qv_q[:].bitcast(FP8X4), scales=qv_s[:], in_=qv_bf[:].rearrange("p q j -> p (q j)"))

        def scores(tags, n, lq, ls, words, bytes_a_col, dt, pl):
            banks = []
            for h in range(T // n):
                bank = ps.tile([P, n], F32, name=tags[h], tag=tags[h])
                nc.tensor.matmul_mx(out=bank[:], lhsT=lq[:].bitcast(FP8X4), lhsT_scale=ls[:],
                                    rhs=words[:, h * n * bytes_a_col:(h + 1) * n * bytes_a_col].bitcast(dt),
                                    rhs_scale=pl[:, h * n:(h + 1) * n], start=True, stop=True)
                banks.append(bank)
            return banks

        a_ps = scores(["a0", "a1", "a2", "a3"], 256, qv_q, qv_s, keys, 2, FP4X4, keys_plane)
        a_sb = sb.tile([P, T], F32, name="a_sb")
        for j in range(4):
            cols = slice(j * 256, (j + 1) * 256)
            if j % 2 == 0:
                nc.scalar.activation(a_sb[:, cols], a_ps[j][:], COPY)
            else:
                nc.vector.tensor_copy(out=a_sb[:, cols], in_=a_ps[j][:])
        b_ps = scores(["b0", "b1"], BANK, qv_q, qv_s, notes, 1, FP8X4, notes_plane)
        c_ps = scores(["c0", "qv_ps"], BANK, st_q, st_s, users, 2, FP4X4, users_plane)

        def pick(name, window, lst):
            picked = sb.tile([P, I], F32, name=name)
            nc.vector.tensor_copy(picked[:, 0:HALF], window[:].indirect(lst[:, 0:HALF_COLS]))
            nc.scalar.activation(picked[:, HALF:I], window[:].indirect(lst[:, HALF_COLS:LIST_COLS]), COPY)
            return picked

        def tail_in_sbuf(name, banks):
            t = sb.tile([P, T - SPLIT], F32, name=name)
            nc.scalar.activation(t[:], banks[1][:, SPLIT - BANK:BANK], COPY)
            return t[:]

        window = a_sb
        for h, (src_list, dst_list) in enumerate(((l1, l2), (l3, l4), (l5, l6))):
            picked = pick("pick%d" % h, window, src_list)
            banks, op = ((b_ps, ADD), (c_ps, ADD), (a_ps, SUB))[h]
            tail = a_sb[:, SPLIT:T] if banks is a_ps else tail_in_sbuf("tail%d" % h, banks)
            nc.vector.tensor_copy(fills[h][:].indirect(dst_list[:]), picked[:])
            window = sb.tile([P, T], F32, name="sum%d" % h)
            nc.gpsimd.tensor_tensor(window[:, SPLIT:T], tail, fills[h][:, SPLIT:T], op)
            width = T // len(banks)
            for c0 in range(0, SPLIT, width):
                c1 = min(c0 + width, SPLIT)
                nc.vector.tensor_tensor(window[:, c0:c1], banks[c0 // width][:, 0:c1 - c0], fills[h][:, c0:c1], op)
        res = pick("res", window, l1)
        nc.sync.dma_start(out=out[:, 0:HALF], in_=res[:, 0:HALF])
        nc.scalar.dma_start(out=out[:, HALF:I], in_=res[:, HALF:I])
